import numpy as np
import ml_dtypes


def mxq(x, axis, fmt="e4m3"):
    dtype, down = {"e4m3": (ml_dtypes.float8_e4m3fn, 7), "e5m2": (ml_dtypes.float8_e5m2, 14)}[fmt]
    v = np.moveaxis(np.asarray(x, np.float32).astype(ml_dtypes.bfloat16).astype(np.float64), axis, -1)
    blocks = v.reshape(v.shape[:-1] + (-1, 32))
    amax = np.abs(blocks).max(-1, keepdims=True)
    byte = np.maximum(np.where(amax > 0, np.frexp(amax)[1] - 1 + 127, 0) - down, 1)
    scale = np.exp2(byte - 127.0)
    codes = (blocks / scale).astype(np.float32).astype(dtype).astype(np.float64)
    return np.moveaxis((codes * scale).reshape(v.shape), -1, axis)


WIDE = False


def mx_kscale(k):
    if not WIDE:
        return np.ones(k)
    levels = np.array([30, -30])
    if k % 512:
        return np.exp2(np.random.permutation(np.resize(levels, k // 32))).repeat(32)
    a = np.empty((k // 512, 16))
    for p in range(k // 512):
        a[p, :8] = np.random.permutation(np.resize(levels, 8))
        for g in range(8):
            far = levels[np.abs(levels - a[p, g]) >= 10]
            a[p, g + 8] = far[np.random.randint(len(far))]
    return np.exp2(a.ravel()).repeat(32)


def f64(x):
    return np.asarray(x).astype(np.float64)


def striped(idx):
    return np.tile(np.asarray(idx).reshape(-1, 16).T, (8, 1)).astype(np.uint16)


def unstriped(offs):
    return offs[:16].T.reshape(-1).astype(np.int64)


E2M1 = np.array([0.0, 0.5, 1.0, 1.5, 2.0, 3.0, 4.0, 6.0, -0.0, -0.5, -1.0, -1.5, -2.0, -3.0, -4.0, -6.0])


def pack_weight(w, fmt):
    k, n = w.shape
    w = f64(np.asarray(w, np.float32).astype(ml_dtypes.bfloat16)).reshape(k // 32, 32, n)
    amax = np.abs(w).max(1)
    if fmt in ("e4m3", "e5m2"):
        byte = np.frexp(amax)[1] - 1 + 127 - (7 if fmt == "e4m3" else 14)
    else:
        mant, ex = np.frexp(amax / 6.0)
        byte = np.where(mant > 0.5, ex, ex - 1) + 127
    byte = np.clip(np.where(amax > 0, byte, 1), 1, 254)
    scaled = (w * np.exp2(127.0 - byte)[:, None, :]).reshape(k, n).astype(np.float32)
    by_word = np.ascontiguousarray(scaled.reshape(k // 512, 128, 4, n).transpose(0, 1, 3, 2))
    if fmt in ("e4m3", "e5m2"):
        words = by_word.astype(ml_dtypes.float8_e4m3fn if fmt == "e4m3" else ml_dtypes.float8_e5m2).view(np.uint8)
    else:
        c = by_word.astype(ml_dtypes.float4_e2m1fn).view(np.uint8) & 0xF
        words = (c[..., 0::2] | (c[..., 1::2] << 4)).reshape(k // 512, 128, 2 * n)
    return np.ascontiguousarray(words), np.ascontiguousarray(byte.astype(np.uint8).reshape(k // 512, 16, n))


def unpack_weight(words, scales, fmt):
    g, _, n = scales.shape
    words = np.ascontiguousarray(words).reshape(g, 128, n, -1)
    if fmt in ("e4m3", "e5m2"):
        vals = words.view(ml_dtypes.float8_e4m3fn if fmt == "e4m3" else ml_dtypes.float8_e5m2).astype(np.float64)
    else:
        nib = np.empty((g, 128, n, 4), np.uint8)
        nib[..., 0::2] = words & 0xF
        nib[..., 1::2] = words >> 4
        vals = E2M1[nib]
    vals = vals * np.repeat(np.exp2(scales.astype(np.float64) - 127.0), 8, axis=1)[..., None]
    return vals.transpose(0, 1, 3, 2).reshape(g * 512, n)


K, T, J, R, N, E = 512, 1024, 256, 512, 256, 1024


def setup_inputs():
    n = np.random.standard_normal
    idx = np.random.permutation(T)[:J]
    idx2 = np.random.permutation(J)[:J]
    idx3 = np.random.permutation(J)[:J]
    idx4 = np.random.permutation(T)[:J]
    idx5 = np.random.permutation(E)[:J]
    fk = mx_kscale(K)
    fr = mx_kscale(R)
    xtp = pack_weight(n((K, T)) / fk[:, None], "e5m2")
    wp = pack_weight(n((K, R)) * 1 / np.sqrt(K) * fk[:, None] * fr, "e2m1")
    wbp = pack_weight(n((R, N)) * 1 / np.sqrt(R) / fr[:, None], "e2m1")
    wsp = pack_weight(n((K, N)) * 1 / np.sqrt(K) * fk[:, None], "e2m1")
    return {
        "xt_words": xtp[0],
        "xt_scales": xtp[1],
        "w_words": wp[0],
        "w_scales": wp[1],
        "wb_words": wbp[0],
        "wb_scales": wbp[1],
        "ws_words": wsp[0],
        "ws_scales": wsp[1],
        "offs": striped(idx),
        "offs2": striped(idx2),
        "offs3": striped(idx3),
        "offs4": striped(idx4),
        "offs5": striped(idx5),
    }


def reference(xt_words, xt_scales, w_words, w_scales, wb_words, wb_scales, ws_words, ws_scales, offs, offs2, offs3, offs4, offs5):
    idx = unstriped(offs)
    idx2 = unstriped(offs2)
    idx3 = unstriped(offs3)
    idx4 = unstriped(offs4)
    idx5 = unstriped(offs5)
    xtu = unpack_weight(xt_words, xt_scales, "e5m2")
    wu = unpack_weight(w_words, w_scales, "e2m1")
    wbu = unpack_weight(wb_words, wb_scales, "e2m1")
    wsu = unpack_weight(ws_words, ws_scales, "e2m1")
    xtidxg = xtu[:, idx]
    a = wu.T @ xtidxg
    h1 = np.maximum(a, a[:, idx2])
    hid = np.abs(h1 - h1[:, idx3])
    hidq = mxq(hid, 0, "e4m3")
    xtidx4g = xtu[:, idx4]
    p = wbu.T @ hidq + wsu.T @ xtidx4g
    y = np.zeros((N, E))
    y[:, idx5] = p
    return y

@@ -1,0 +1,196 @@
+from contextlib import ExitStack
+
+import concourse.mybir as mybir
+
+K, T, J, R, N, E = 512, 1024, 256, 512, 256, 1024
+FLOPS = 2 * K * R * J + 2 * R * N * J + 2 * K * N * J
+
+F32 = mybir.dt.float32
+BF16 = mybir.dt.bfloat16
+I32 = mybir.dt.int32
+U32 = mybir.dt.uint32
+U16 = mybir.dt.uint16
+U8 = mybir.dt.uint8
+E4M3X4 = mybir.dt.float8_e4m3fn_x4
+E5M2X4 = mybir.dt.float8_e5m2_x4
+E2M1X4 = mybir.dt.float4_e2m1fn_x4
+ACT = mybir.ActivationFunctionType
+ALU = mybir.AluOpType
+
+P = 128
+PACK = 4
+HALF = J // 2
+SPARE = 96
+
+
+def load_scales(queue, plane, rows, quadrants=(0, 1, 2, 3)):
+    words = rows.bitcast(I32)
+    for q in quadrants:
+        queue.dma_start(plane[32 * q : 32 * q + 4, :].bitcast(I32), words[4 * q : 4 * (q + 1), :])
+
+
+def load_scale_part(queue, plane, rows, upper):
+    words = rows.bitcast(I32)
+    first_row, count, first_partition, copies = (12, 4, 84, 11) if upper else (0, 14, 0, 6)
+    run = words[first_row : first_row + count, :]
+    queue.dma_start(
+        plane[first_partition : first_partition + count * copies, :].bitcast(I32),
+        run.unsqueeze(0).broadcast_to([copies, count, words.shape[1]]),
+    )
+
+
+def tile_list_passedon_solo_further_scattered_kernel(
+    tc, xt_words, xt_scales, w_words, w_scales, wb_words, wb_scales, ws_words, ws_scales,
+    offs, offs2, offs3, offs4, offs5, out
+):
+    nc = tc.nc
+    with ExitStack() as ctx:
+        keep = ctx.enter_context(tc.tile_pool(name="keep", bufs=1))
+        psum = ctx.enter_context(tc.psum_pool(name="psum", bufs=1))
+
+        def sb(name, shape, dtype):
+            return keep.tile(shape, dtype, name=name, align_bytes=64)
+
+        idx = sb("idx", [P, J // 16], U16)
+        idx2 = sb("idx2", [P, J // 16], U16)
+        idx3 = sb("idx3", [P, J // 16], U16)
+        idx4 = sb("idx4", [P, J // 16], U16)
+        idx5 = sb("idx5", [P, J // 16], U16)
+        xw = sb("xw", [P, T], I32)
+        xs = sb("xs", [P, T], U8)
+        ww = sb("ww", [P, 2 * R], U8)
+        wsc = sb("wsc", [P, R], U8)
+        wbw = sb("wbw", [P, 2 * N], U8)
+        wbs = sb("wbs", [P, N], U8)
+        wsw = sb("wsw", [P, 2 * N], U8)
+        wss = sb("wss", [P, N], U8)
+
+        nc.sync.dma_start(idx[:], offs)
+        nc.scalar.dma_start(xw[:], xt_words[0].rearrange("p c r -> p (c r)").bitcast(I32))
+        load_scale_part(nc.sync, xs, xt_scales[0], True)
+        load_scale_part(nc.scalar, xs, xt_scales[0], False)
+        nc.sync.dma_start(ww[:].bitcast(I32), w_words[0].bitcast(I32))
+        load_scale_part(nc.sync, wsc, w_scales[0], True)
+        load_scale_part(nc.scalar, wsc, w_scales[0], False)
+        nc.sync.dma_start(idx4[:], offs4)
+        nc.sync.dma_start(idx2[:], offs2)
+        nc.sync.dma_start(idx3[:], offs3)
+        nc.sync.dma_start(wsw[:].bitcast(I32), ws_words[0].bitcast(I32))
+        load_scales(nc.sync, wss, ws_scales[0])
+        nc.sync.dma_start(wbw[:].bitcast(I32), wb_words[0].bitcast(I32))
+        load_scales(nc.sync, wbs, wb_scales[0])
+        nc.sync.dma_start(idx5[:], offs5)
+
+        pages = [sb("page%d" % n, [P, E], F32) for n in range(2)]
+        a = [sb("a%d" % t, [P, J + SPARE], F32) for t in range(PACK)]
+        for page in pages:
+            nc.vector.memset(page[:], 0.0)
+        for t in range(PACK):
+            nc.vector.memset(a[t][:, J:], 0.0)
+
+        wd = sb("wd", [P, PACK, 2 * P], U8)
+        wds = sb("wds", [P, PACK, P], U8)
+        nc.vector.tensor_copy(out=wds[:], in_=wsc[:].rearrange("p (m t) -> p t m", t=PACK))
+        nc.scalar.copy(out=wd[:].bitcast(U16), in_=ww[:].bitcast(U16).rearrange("p (m t) -> p t m", t=PACK))
+
+        xg = sb("xg", [P, J], U32)
+        xgs = sb("xgs", [P, J], U8)
+        xg4 = sb("xg4", [P, J], U32)
+        xgs4 = sb("xgs4", [P, J], U8)
+        nc.vector.tensor_copy(xgs[:], xs[:].indirect(idx[:]))
+        nc.vector.tensor_copy(xgs4[:], xs[:].indirect(idx4[:]))
+        nc.vector.tensor_copy(xg[:], xw[:].bitcast(U32).indirect(idx[:]))
+        nc.vector.tensor_copy(xg4[:], xw[:].bitcast(U32).indirect(idx4[:]))
+
+        acc = [psum.tile([P, J], F32, name="acc%d" % t) for t in range(PACK)]
+        for t in range(PACK):
+            nc.tensor.matmul_mx(
+                out=acc[t][:], lhsT=wd[:, t, :].bitcast(E2M1X4), lhsT_scale=wds[:, t, :],
+                rhs=xg[:].bitcast(E5M2X4), rhs_scale=xgs[:], start=True, stop=True,
+            )
+        res = [[psum.tile([P, HALF], F32, name="res%d%d" % (u, n)) for n in range(2)] for u in range(2)]
+        for u in range(2):
+            for n in range(2):
+                nc.tensor.matmul_mx(
+                    out=res[u][n][:], lhsT=wsw[:, 2 * P * n : 2 * P * (n + 1)].bitcast(E2M1X4),
+                    lhsT_scale=wss[:, P * n : P * (n + 1)],
+                    rhs=xg4[:, HALF * u : HALF * (u + 1)].bitcast(E5M2X4),
+                    rhs_scale=xgs4[:, HALF * u : HALF * (u + 1)], start=True, stop=False,
+                )
+
+        g2 = sb("g2", [P, PACK, J], F32)
+        h = sb("h", [P, PACK, J], F32)
+        g3 = [sb("g3%d" % u, [P, PACK, HALF], F32) for u in range(2)]
+        d = [sb("d%d" % u, [P, PACK, HALF], F32) for u in range(2)]
+        hid = [sb("hid%d" % u, [P, HALF, PACK], BF16) for u in range(2)]
+        hq = [sb("hq%d" % u, [P, HALF], U32) for u in range(2)]
+        hs = [sb("hs%d" % u, [P, HALF], U8) for u in range(2)]
+        p = [[sb("p%d%d" % (u, n), [P, HALF], F32) for n in range(2)] for u in range(2)]
+
+        def gather(on_vector, dst, window, offsets):
+            if on_vector:
+                nc.vector.tensor_copy(dst, window.indirect(offsets))
+            else:
+                nc.scalar.activation(dst, window.indirect(offsets), ACT.Copy)
+
+        def half(lst, u):
+            return lst[:, 8 * u : 8 * (u + 1)]
+
+        def pick3(on_vector, t, u):
+            gather(on_vector, g3[u][:, t, :], h[:, t, :], half(idx3, u))
+
+        def subtract(u, t0, t1):
+            nc.vector.tensor_tensor(
+                d[u][:, t0:t1, :], h[:, t0:t1, HALF * u : HALF * (u + 1)], g3[u][:, t0:t1, :], ALU.subtract
+            )
+
+        def magnitude(u):
+            nc.scalar.activation(
+                hid[u][:].rearrange("p (c i) t -> p c t i", i=4),
+                d[u][:].rearrange("p t (c i) -> p c t i", i=4),
+                ACT.Abs,
+            )
+
+        def quantise(u):
+            nc.vector.quantize_mx(
+                out=hq[u][:].bitcast(E4M3X4), scales=hs[u][:], in_=hid[u][:].rearrange("p j t -> p (j t)")
+            )
+
+        def second(u):
+            for n in range(2):
+                nc.tensor.matmul_mx(
+                    out=res[u][n][:], lhsT=wbw[:, 2 * P * n : 2 * P * (n + 1)].bitcast(E2M1X4),
+                    lhsT_scale=wbs[:, P * n : P * (n + 1)],
+                    rhs=hq[u][:].bitcast(E4M3X4), rhs_scale=hs[u][:], start=False, stop=True,
+                )
+
+        def place(u):
+            nc.vector.tensor_copy(p[u][0][:], res[u][0][:])
+            nc.scalar.copy(p[u][1][:], res[u][1][:])
+            nc.vector.tensor_copy(pages[0][:].indirect(half(idx5, u)), p[u][0][:])
+            nc.scalar.activation(pages[1][:].indirect(half(idx5, u)), p[u][1][:], ACT.Copy)
+
+        for t in range(PACK):
+            nc.scalar.copy(a[t][:, :J], acc[t][:])
+        for t in range(PACK):
+            gather(t < 2, g2[:, t, :], a[t][:], idx2[:])
+        for t in range(PACK):
+            nc.vector.tensor_tensor(h[:, t, :], a[t][:, :J], g2[:, t, :], ALU.max)
+        for t in range(PACK):
+            pick3(t >= 2, t, 0)
+        subtract(0, 0, 2)
+        subtract(0, 2, 4)
+        for t in range(PACK):
+            pick3(False, t, 1)
+        magnitude(0)
+        subtract(1, 0, 4)
+        quantise(0)
+        magnitude(1)
+        second(0)
+        quantise(1)
+        second(1)
+        place(0)
+        place(1)
+
+        nc.sync.dma_start(out[0:P, :], pages[0][:])
+        nc.scalar.dma_start(out[P : 2 * P, :], pages[1][:])

@@ -23,10 +23,14 @@ HALF = J // 2
 SPARE = 96
 
 
-def load_scales(queue, plane, rows, quadrants=(0, 1, 2, 3)):
+def load_scales(queue, plane, rows, fill=False, quadrants=(0, 1, 2, 3)):
     words = rows.bitcast(I32)
     for q in quadrants:
-        queue.dma_start(plane[32 * q : 32 * q + 4, :].bitcast(I32), words[4 * q : 4 * (q + 1), :])
+        four = words[4 * q : 4 * (q + 1), :]
+        if fill:
+            queue.dma_start(plane[32 * q : 32 * (q + 1), :].bitcast(I32), four.unsqueeze(0).broadcast_to([8, 4, words.shape[1]]))
+        else:
+            queue.dma_start(plane[32 * q : 32 * q + 4, :].bitcast(I32), four)
 
 
 def load_scale_part(queue, plane, rows, upper):
@@ -48,8 +52,8 @@ def tile_list_passedon_solo_further_scattered_kernel(
         keep = ctx.enter_context(tc.tile_pool(name="keep", bufs=1))
         psum = ctx.enter_context(tc.psum_pool(name="psum", bufs=1))
 
-        def sb(name, shape, dtype):
-            return keep.tile(shape, dtype, name=name, align_bytes=64)
+        def sb(name, shape, dtype, tag=None):
+            return keep.tile(shape, dtype, name=name, tag=tag or name, align_bytes=64)
 
         idx = sb("idx", [P, J // 16], U16)
         idx2 = sb("idx2", [P, J // 16], U16)
@@ -67,11 +71,10 @@ def tile_list_passedon_solo_further_scattered_kernel(
 
         nc.sync.dma_start(idx[:], offs)
         nc.scalar.dma_start(xw[:], xt_words[0].rearrange("p c r -> p (c r)").bitcast(I32))
-        load_scale_part(nc.sync, xs, xt_scales[0], True)
-        load_scale_part(nc.scalar, xs, xt_scales[0], False)
-        nc.sync.dma_start(ww[:].bitcast(I32), w_words[0].bitcast(I32))
-        load_scale_part(nc.sync, wsc, w_scales[0], True)
+        nc.gpsimd.dma_start(ww[:].bitcast(I32), w_words[0].bitcast(I32))
+        load_scales(nc.sync, xs, xt_scales[0], True)
         load_scale_part(nc.scalar, wsc, w_scales[0], False)
+        load_scale_part(nc.sync, wsc, w_scales[0], True)
         nc.sync.dma_start(idx4[:], offs4)
         nc.sync.dma_start(idx2[:], offs2)
         nc.sync.dma_start(idx3[:], offs3)
@@ -83,34 +86,40 @@ def tile_list_passedon_solo_further_scattered_kernel(
 
         pages = [sb("page%d" % n, [P, E], F32) for n in range(2)]
         a = [sb("a%d" % t, [P, J + SPARE], F32) for t in range(PACK)]
-        for page in pages:
-            nc.vector.memset(page[:], 0.0)
         for t in range(PACK):
-            nc.vector.memset(a[t][:, J:], 0.0)
+            nc.gpsimd.memset(a[t][:, J:], 0.0)
+        nc.gpsimd.memset(pages[0][:], 0.0)
+        nc.vector.memset(pages[1][:, : E - 1], 0.0)
+        nc.vector.memset(pages[1][:, E - 1 :], 0.0)
 
-        wd = sb("wd", [P, PACK, 2 * P], U8)
-        wds = sb("wds", [P, PACK, P], U8)
-        nc.vector.tensor_copy(out=wds[:], in_=wsc[:].rearrange("p (m t) -> p t m", t=PACK))
-        nc.scalar.copy(out=wd[:].bitcast(U16), in_=ww[:].bitcast(U16).rearrange("p (m t) -> p t m", t=PACK))
+        wd = [sb("wd%d" % t, [P, 2 * P], U8) for t in range(PACK)]
+        wds = [sb("wds%d" % t, [P, P], U8) for t in range(PACK)]
+        for t in range(PACK):
+            nc.scalar.copy(out=wd[t][:].bitcast(U16), in_=ww[:].bitcast(U16)[:, t::PACK])
 
         xg = sb("xg", [P, J], U32)
         xgs = sb("xgs", [P, J], U8)
         xg4 = sb("xg4", [P, J], U32)
         xgs4 = sb("xgs4", [P, J], U8)
         nc.vector.tensor_copy(xgs[:], xs[:].indirect(idx[:]))
-        nc.vector.tensor_copy(xgs4[:], xs[:].indirect(idx4[:]))
-        nc.vector.tensor_copy(xg[:], xw[:].bitcast(U32).indirect(idx[:]))
-        nc.vector.tensor_copy(xg4[:], xw[:].bitcast(U32).indirect(idx4[:]))
+        nc.vector.tensor_copy(xg[:, :HALF], xw[:].bitcast(U32).indirect(idx[:, 0:8]))
+        nc.vector.tensor_copy(out=wds[0][:], in_=wsc[:, 0::PACK])
+        nc.vector.tensor_copy(xg[:, HALF:], xw[:].bitcast(U32).indirect(idx[:, 8:16]))
+        for t in range(1, PACK):
+            nc.vector.tensor_copy(out=wds[t][:], in_=wsc[:, t::PACK])
 
         acc = [psum.tile([P, J], F32, name="acc%d" % t) for t in range(PACK)]
         for t in range(PACK):
-            nc.tensor.matmul_mx(
-                out=acc[t][:], lhsT=wd[:, t, :].bitcast(E2M1X4), lhsT_scale=wds[:, t, :],
-                rhs=xg[:].bitcast(E5M2X4), rhs_scale=xgs[:], start=True, stop=True,
-            )
+            for u in range(2):
+                cols = slice(HALF * u, HALF * (u + 1))
+                nc.tensor.matmul_mx(
+                    out=acc[t][:, cols], lhsT=wd[t][:].bitcast(E2M1X4), lhsT_scale=wds[t][:],
+                    rhs=xg[:, cols].bitcast(E5M2X4), rhs_scale=xgs[:, cols], start=True, stop=True,
+                )
         res = [[psum.tile([P, HALF], F32, name="res%d%d" % (u, n)) for n in range(2)] for u in range(2)]
-        for u in range(2):
-            for n in range(2):
+
+        def short_way(u):
+            for n in (1, 0):
                 nc.tensor.matmul_mx(
                     out=res[u][n][:], lhsT=wsw[:, 2 * P * n : 2 * P * (n + 1)].bitcast(E2M1X4),
                     lhsT_scale=wss[:, P * n : P * (n + 1)],
@@ -118,10 +127,10 @@ def tile_list_passedon_solo_further_scattered_kernel(
                     rhs_scale=xgs4[:, HALF * u : HALF * (u + 1)], start=True, stop=False,
                 )
 
-        g2 = sb("g2", [P, PACK, J], F32)
+        g2 = [sb("g2%d" % t, [P, J], F32) for t in range(PACK)]
         h = sb("h", [P, PACK, J], F32)
-        g3 = [sb("g3%d" % u, [P, PACK, HALF], F32) for u in range(2)]
-        d = [sb("d%d" % u, [P, PACK, HALF], F32) for u in range(2)]
+        g3 = {}
+        d = {}
         hid = [sb("hid%d" % u, [P, HALF, PACK], BF16) for u in range(2)]
         hq = [sb("hq%d" % u, [P, HALF], U32) for u in range(2)]
         hs = [sb("hs%d" % u, [P, HALF], U8) for u in range(2)]
@@ -137,11 +146,11 @@ def tile_list_passedon_solo_further_scattered_kernel(
             return lst[:, 8 * u : 8 * (u + 1)]
 
         def pick3(on_vector, t, u):
-            gather(on_vector, g3[u][:, t, :], h[:, t, :], half(idx3, u))
+            gather(on_vector, g3[u][t], h[:, t, :], half(idx3, u))
 
         def subtract(u, t0, t1):
             nc.vector.tensor_tensor(
-                d[u][:, t0:t1, :], h[:, t0:t1, HALF * u : HALF * (u + 1)], g3[u][:, t0:t1, :], ALU.subtract
+                d[u][:, t0:t1, :], h[:, t0:t1, HALF * u : HALF * (u + 1)], g3pair[u][t0 // 2], ALU.subtract
             )
 
         def magnitude(u):
@@ -157,40 +166,66 @@ def tile_list_passedon_solo_further_scattered_kernel(
             )
 
         def second(u):
-            for n in range(2):
+            for n in (1, 0):
                 nc.tensor.matmul_mx(
                     out=res[u][n][:], lhsT=wbw[:, 2 * P * n : 2 * P * (n + 1)].bitcast(E2M1X4),
                     lhsT_scale=wbs[:, P * n : P * (n + 1)],
                     rhs=hq[u][:].bitcast(E4M3X4), rhs_scale=hs[u][:], start=False, stop=True,
                 )
 
-        def place(u):
-            nc.vector.tensor_copy(p[u][0][:], res[u][0][:])
-            nc.scalar.copy(p[u][1][:], res[u][1][:])
-            nc.vector.tensor_copy(pages[0][:].indirect(half(idx5, u)), p[u][0][:])
-            nc.scalar.activation(pages[1][:].indirect(half(idx5, u)), p[u][1][:], ACT.Copy)
+        def empty(on_vector, u, n):
+            if on_vector:
+                nc.vector.tensor_copy(p[u][n][:], res[u][n][:])
+            else:
+                nc.scalar.copy(p[u][n][:], res[u][n][:])
 
+        def place(on_vector, u, n):
+            if on_vector:
+                nc.vector.tensor_copy(pages[n][:].indirect(half(idx5, u)), p[u][n][:])
+            else:
+                nc.scalar.activation(pages[n][:].indirect(half(idx5, u)), p[u][n][:], ACT.Copy)
+
+        nc.vector.tensor_copy(xg4[:], xw[:].bitcast(U32).indirect(idx4[:]))
+        nc.vector.tensor_copy(xgs4[:], xs[:].indirect(idx4[:]))
         for t in range(PACK):
             nc.scalar.copy(a[t][:, :J], acc[t][:])
         for t in range(PACK):
-            gather(t < 2, g2[:, t, :], a[t][:], idx2[:])
+            gather(t < 2, g2[t][:], a[t][:], idx2[:])
         for t in range(PACK):
-            nc.vector.tensor_tensor(h[:, t, :], a[t][:, :J], g2[:, t, :], ALU.max)
+            nc.vector.tensor_tensor(h[:, t, :], a[t][:, :J], g2[t][:], ALU.max)
+        short_way(0)
+        short_way(1)
+        g3pair = {}
+        g30 = sb("g30", [P, PACK, HALF], F32)
+        g3[0] = [g30[:, t, :] for t in range(PACK)]
+        g3pair[0] = [g30[:, 0:2, :], g30[:, 2:4, :]]
+        d[0] = sb("d0", [P, PACK, HALF], F32)
         for t in range(PACK):
-            pick3(t >= 2, t, 0)
+            pick3(t == 2, t, 0)
         subtract(0, 0, 2)
         subtract(0, 2, 4)
+        g31 = [sb("g31%d" % k, [P, 2, HALF], F32, tag="g2%d" % (2 + k)) for k in range(2)]
+        g3[1] = [g31[t // 2][:, t % 2, :] for t in range(PACK)]
+        g3pair[1] = [g31[0][:], g31[1][:]]
+        d[1] = sb("d1", [P, PACK, HALF], F32, tag="g30")
         for t in range(PACK):
-            pick3(False, t, 1)
+            pick3(t == 0, t, 1)
         magnitude(0)
-        subtract(1, 0, 4)
+        subtract(1, 0, 2)
+        subtract(1, 2, 4)
         quantise(0)
         magnitude(1)
         second(0)
         quantise(1)
+        empty(False, 0, 1)
+        place(False, 0, 1)
+        empty(True, 0, 0)
         second(1)
-        place(0)
-        place(1)
+        empty(True, 1, 1)
+        empty(True, 1, 0)
+        place(False, 0, 0)
+        place(True, 1, 1)
+        place(False, 1, 0)
 
-        nc.sync.dma_start(out[0:P, :], pages[0][:])
-        nc.scalar.dma_start(out[P : 2 * P, :], pages[1][:])
+        nc.sync.dma_start(out[P : 2 * P, :], pages[1][:])
+        nc.scalar.dma_start(out[0:P, :], pages[0][:])

@@ -19,27 +19,27 @@ ALU = mybir.AluOpType
 
 P = 128
 PACK = 4
+QUADRANT = 32
 HALF = J // 2
+LIST_COLUMNS = J // 16
 SPARE = 96
+PAGE_ORDER = (1, 0)
+VECTOR_PLANES_OF_A = 2
+VECTOR_PLANE_OF_H1 = (2, 0)
 
 
-def load_scales(queue, plane, rows, fill=False, quadrants=(0, 1, 2, 3)):
+def load_scale_rows(queue, tile, rows):
     words = rows.bitcast(I32)
-    for q in quadrants:
-        four = words[4 * q : 4 * (q + 1), :]
-        if fill:
-            queue.dma_start(plane[32 * q : 32 * (q + 1), :].bitcast(I32), four.unsqueeze(0).broadcast_to([8, 4, words.shape[1]]))
-        else:
-            queue.dma_start(plane[32 * q : 32 * q + 4, :].bitcast(I32), four)
+    for quadrant in range(P // QUADRANT):
+        first = QUADRANT * quadrant
+        queue.dma_start(tile[first : first + 4, :].bitcast(I32), words[4 * quadrant : 4 * quadrant + 4, :])
 
 
-def load_scale_part(queue, plane, rows, upper):
-    words = rows.bitcast(I32)
-    first_row, count, first_partition, copies = (12, 4, 84, 11) if upper else (0, 14, 0, 6)
-    run = words[first_row : first_row + count, :]
+def load_repeated_rows(queue, tile, rows, first_partition, first_row, count, copies):
+    words = rows.bitcast(I32)[first_row : first_row + count, :]
     queue.dma_start(
-        plane[first_partition : first_partition + count * copies, :].bitcast(I32),
-        run.unsqueeze(0).broadcast_to([copies, count, words.shape[1]]),
+        tile[first_partition : first_partition + count * copies, :].bitcast(I32),
+        words.unsqueeze(0).broadcast_to([copies, count, words.shape[1]]),
     )
 
 
@@ -52,180 +52,180 @@ def tile_list_passedon_solo_further_scattered_kernel(
         keep = ctx.enter_context(tc.tile_pool(name="keep", bufs=1))
         psum = ctx.enter_context(tc.psum_pool(name="psum", bufs=1))
 
-        def sb(name, shape, dtype, tag=None):
-            return keep.tile(shape, dtype, name=name, tag=tag or name, align_bytes=64)
+        def sbuf(name, shape, dtype, on_bytes_of=None):
+            return keep.tile(shape, dtype, name=name, tag=on_bytes_of or name, align_bytes=64)
 
-        idx = sb("idx", [P, J // 16], U16)
-        idx2 = sb("idx2", [P, J // 16], U16)
-        idx3 = sb("idx3", [P, J // 16], U16)
-        idx4 = sb("idx4", [P, J // 16], U16)
-        idx5 = sb("idx5", [P, J // 16], U16)
-        xw = sb("xw", [P, T], I32)
-        xs = sb("xs", [P, T], U8)
-        ww = sb("ww", [P, 2 * R], U8)
-        wsc = sb("wsc", [P, R], U8)
-        wbw = sb("wbw", [P, 2 * N], U8)
-        wbs = sb("wbs", [P, N], U8)
-        wsw = sb("wsw", [P, 2 * N], U8)
-        wss = sb("wss", [P, N], U8)
+        def half_of(offsets, u):
+            return offsets[:, u * LIST_COLUMNS // 2 : (u + 1) * LIST_COLUMNS // 2]
+
+        def slots(u):
+            return slice(HALF * u, HALF * (u + 1))
+
+        idx = sbuf("idx", [P, LIST_COLUMNS], U16)
+        idx2 = sbuf("idx2", [P, LIST_COLUMNS], U16)
+        idx3 = sbuf("idx3", [P, LIST_COLUMNS], U16)
+        idx4 = sbuf("idx4", [P, LIST_COLUMNS], U16)
+        idx5 = sbuf("idx5", [P, LIST_COLUMNS], U16)
+        xt_w = sbuf("xt_w", [P, T], I32)
+        xt_s = sbuf("xt_s", [P, T], U8)
+        w_w = sbuf("w_w", [P, 2 * R], U8)
+        w_s = sbuf("w_s", [P, R], U8)
+        wb_w = sbuf("wb_w", [P, 2 * N], U8)
+        wb_s = sbuf("wb_s", [P, N], U8)
+        ws_w = sbuf("ws_w", [P, 2 * N], U8)
+        ws_s = sbuf("ws_s", [P, N], U8)
 
         nc.sync.dma_start(idx[:], offs)
-        nc.scalar.dma_start(xw[:], xt_words[0].rearrange("p c r -> p (c r)").bitcast(I32))
-        nc.gpsimd.dma_start(ww[:].bitcast(I32), w_words[0].bitcast(I32))
-        load_scales(nc.sync, xs, xt_scales[0], True)
-        load_scale_part(nc.scalar, wsc, w_scales[0], False)
-        load_scale_part(nc.sync, wsc, w_scales[0], True)
+        nc.scalar.dma_start(xt_w[:], xt_words[0].rearrange("p c r -> p (c r)").bitcast(I32))
+        nc.gpsimd.dma_start(w_w[:].bitcast(I32), w_words[0].bitcast(I32))
+        for quadrant in range(P // QUADRANT):
+            load_repeated_rows(nc.sync, xt_s, xt_scales[0], QUADRANT * quadrant, 4 * quadrant, 4, QUADRANT // 4)
+        load_repeated_rows(nc.scalar, w_s, w_scales[0], 0, 0, 14, 6)
+        load_repeated_rows(nc.sync, w_s, w_scales[0], 84, 12, 4, 11)
         nc.sync.dma_start(idx4[:], offs4)
         nc.sync.dma_start(idx2[:], offs2)
         nc.sync.dma_start(idx3[:], offs3)
-        nc.sync.dma_start(wsw[:].bitcast(I32), ws_words[0].bitcast(I32))
-        load_scales(nc.sync, wss, ws_scales[0])
-        nc.sync.dma_start(wbw[:].bitcast(I32), wb_words[0].bitcast(I32))
-        load_scales(nc.sync, wbs, wb_scales[0])
+        nc.sync.dma_start(ws_w[:].bitcast(I32), ws_words[0].bitcast(I32))
+        load_scale_rows(nc.sync, ws_s, ws_scales[0])
+        nc.sync.dma_start(wb_w[:].bitcast(I32), wb_words[0].bitcast(I32))
+        load_scale_rows(nc.sync, wb_s, wb_scales[0])
         nc.sync.dma_start(idx5[:], offs5)
 
-        pages = [sb("page%d" % n, [P, E], F32) for n in range(2)]
-        a = [sb("a%d" % t, [P, J + SPARE], F32) for t in range(PACK)]
+        pages = [sbuf("page%d" % n, [P, E], F32) for n in range(2)]
+        a = [sbuf("a%d" % t, [P, J + SPARE], F32) for t in range(PACK)]
         for t in range(PACK):
             nc.gpsimd.memset(a[t][:, J:], 0.0)
         nc.gpsimd.memset(pages[0][:], 0.0)
         nc.vector.memset(pages[1][:, : E - 1], 0.0)
         nc.vector.memset(pages[1][:, E - 1 :], 0.0)
 
-        wd = [sb("wd%d" % t, [P, 2 * P], U8) for t in range(PACK)]
-        wds = [sb("wds%d" % t, [P, P], U8) for t in range(PACK)]
+        dealt_w = [sbuf("dealt_w%d" % t, [P, 2 * P], U8) for t in range(PACK)]
+        dealt_s = [sbuf("dealt_s%d" % t, [P, P], U8) for t in range(PACK)]
         for t in range(PACK):
-            nc.scalar.copy(out=wd[t][:].bitcast(U16), in_=ww[:].bitcast(U16)[:, t::PACK])
+            nc.scalar.copy(out=dealt_w[t][:].bitcast(U16), in_=w_w[:].bitcast(U16)[:, t::PACK])
 
-        xg = sb("xg", [P, J], U32)
-        xgs = sb("xgs", [P, J], U8)
-        xg4 = sb("xg4", [P, J], U32)
-        xgs4 = sb("xgs4", [P, J], U8)
-        nc.vector.tensor_copy(xgs[:], xs[:].indirect(idx[:]))
-        nc.vector.tensor_copy(xg[:, :HALF], xw[:].bitcast(U32).indirect(idx[:, 0:8]))
-        nc.vector.tensor_copy(out=wds[0][:], in_=wsc[:, 0::PACK])
-        nc.vector.tensor_copy(xg[:, HALF:], xw[:].bitcast(U32).indirect(idx[:, 8:16]))
+        def deal_scales(t):
+            nc.vector.tensor_copy(out=dealt_s[t][:], in_=w_s[:, t::PACK])
+
+        xt_window = xt_w[:].bitcast(U32)
+        tok_w = sbuf("tok_w", [P, J], U32)
+        tok_s = sbuf("tok_s", [P, J], U8)
+        short_w = [sbuf("short_w0", [P, HALF], U32)]
+        short_s = [sbuf("short_s0", [P, HALF], U8)]
+        nc.vector.tensor_copy(tok_s[:], xt_s[:].indirect(idx[:]))
+        nc.vector.tensor_copy(tok_w[:, slots(0)], xt_window.indirect(half_of(idx, 0)))
+        deal_scales(0)
+        nc.vector.tensor_copy(tok_w[:, slots(1)], xt_window.indirect(half_of(idx, 1)))
         for t in range(1, PACK):
-            nc.vector.tensor_copy(out=wds[t][:], in_=wsc[:, t::PACK])
+            deal_scales(t)
 
-        acc = [psum.tile([P, J], F32, name="acc%d" % t) for t in range(PACK)]
+        a_bank = [psum.tile([P, J], F32, name="a_bank%d" % t) for t in range(PACK)]
         for t in range(PACK):
             for u in range(2):
-                cols = slice(HALF * u, HALF * (u + 1))
                 nc.tensor.matmul_mx(
-                    out=acc[t][:, cols], lhsT=wd[t][:].bitcast(E2M1X4), lhsT_scale=wds[t][:],
-                    rhs=xg[:, cols].bitcast(E5M2X4), rhs_scale=xgs[:, cols], start=True, stop=True,
-                )
-        res = [[psum.tile([P, HALF], F32, name="res%d%d" % (u, n)) for n in range(2)] for u in range(2)]
-
-        def short_way(u):
-            for n in (1, 0):
-                nc.tensor.matmul_mx(
-                    out=res[u][n][:], lhsT=wsw[:, 2 * P * n : 2 * P * (n + 1)].bitcast(E2M1X4),
-                    lhsT_scale=wss[:, P * n : P * (n + 1)],
-                    rhs=xg4[:, HALF * u : HALF * (u + 1)].bitcast(E5M2X4),
-                    rhs_scale=xgs4[:, HALF * u : HALF * (u + 1)], start=True, stop=False,
+                    out=a_bank[t][:, slots(u)], lhsT=dealt_w[t][:].bitcast(E2M1X4), lhsT_scale=dealt_s[t][:],
+                    rhs=tok_w[:, slots(u)].bitcast(E5M2X4), rhs_scale=tok_s[:, slots(u)], start=True, stop=True,
                 )
 
-        g2 = [sb("g2%d" % t, [P, J], F32) for t in range(PACK)]
-        h = sb("h", [P, PACK, J], F32)
-        g3 = {}
-        d = {}
-        hid = [sb("hid%d" % u, [P, HALF, PACK], BF16) for u in range(2)]
-        hq = [sb("hq%d" % u, [P, HALF], U32) for u in range(2)]
-        hs = [sb("hs%d" % u, [P, HALF], U8) for u in range(2)]
-        p = [[sb("p%d%d" % (u, n), [P, HALF], F32) for n in range(2)] for u in range(2)]
+        p_bank = [[psum.tile([P, HALF], F32, name="p_bank%d%d" % (u, n)) for n in range(2)] for u in range(2)]
+        partner = [sbuf("partner%d" % t, [P, J], F32) for t in range(PACK)]
+        h1 = sbuf("h1", [P, PACK, J], F32)
+        hid = [sbuf("hid%d" % u, [P, HALF, PACK], BF16) for u in range(2)]
+        hid_w = [sbuf("hid_w%d" % u, [P, HALF], U32) for u in range(2)]
+        hid_s = [sbuf("hid_s%d" % u, [P, HALF], U8) for u in range(2)]
+        p = [[sbuf("p%d%d" % (u, n), [P, HALF], F32) for n in range(2)] for u in range(2)]
 
-        def gather(on_vector, dst, window, offsets):
+        def gather_short_tokens(u):
+            nc.vector.tensor_copy(short_w[u][:], xt_window.indirect(half_of(idx4, u)))
+            nc.vector.tensor_copy(short_s[u][:], xt_s[:].indirect(half_of(idx4, u)))
+
+        def look_up(on_vector, picked, window, offsets):
             if on_vector:
-                nc.vector.tensor_copy(dst, window.indirect(offsets))
+                nc.vector.tensor_copy(picked, window.indirect(offsets))
             else:
-                nc.scalar.activation(dst, window.indirect(offsets), ACT.Copy)
+                nc.scalar.activation(picked, window.indirect(offsets), ACT.Copy)
 
-        def half(lst, u):
-            return lst[:, 8 * u : 8 * (u + 1)]
+        def look_up_h1(u, pairs):
+            for t in range(PACK):
+                look_up(t == VECTOR_PLANE_OF_H1[u], pairs[t // 2][:, t % 2, :], h1[:, t, :], half_of(idx3, u))
 
-        def pick3(on_vector, t, u):
-            gather(on_vector, g3[u][t], h[:, t, :], half(idx3, u))
+        def subtract(u, pairs, diff):
+            for i in range(2):
+                planes = slice(2 * i, 2 * i + 2)
+                nc.vector.tensor_tensor(diff[:, planes, :], h1[:, planes, slots(u)], pairs[i], ALU.subtract)
 
-        def subtract(u, t0, t1):
-            nc.vector.tensor_tensor(
-                d[u][:, t0:t1, :], h[:, t0:t1, HALF * u : HALF * (u + 1)], g3pair[u][t0 // 2], ALU.subtract
-            )
-
-        def magnitude(u):
+        def magnitude(u, diff):
             nc.scalar.activation(
-                hid[u][:].rearrange("p (c i) t -> p c t i", i=4),
-                d[u][:].rearrange("p t (c i) -> p c t i", i=4),
+                hid[u][:].rearrange("q (c i) t -> q c t i", i=4),
+                diff[:].rearrange("q t (c i) -> q c t i", i=4),
                 ACT.Abs,
             )
 
         def quantise(u):
             nc.vector.quantize_mx(
-                out=hq[u][:].bitcast(E4M3X4), scales=hs[u][:], in_=hid[u][:].rearrange("p j t -> p (j t)")
+                out=hid_w[u][:].bitcast(E4M3X4), scales=hid_s[u][:], in_=hid[u][:].rearrange("q j t -> q (j t)")
             )
 
-        def second(u):
-            for n in (1, 0):
-                nc.tensor.matmul_mx(
-                    out=res[u][n][:], lhsT=wbw[:, 2 * P * n : 2 * P * (n + 1)].bitcast(E2M1X4),
-                    lhsT_scale=wbs[:, P * n : P * (n + 1)],
-                    rhs=hq[u][:].bitcast(E4M3X4), rhs_scale=hs[u][:], start=False, stop=True,
-                )
+        def pass_with_ws(u, n, first):
+            nc.tensor.matmul_mx(
+                out=p_bank[u][n][:], lhsT=ws_w[:, 2 * P * n : 2 * P * (n + 1)].bitcast(E2M1X4),
+                lhsT_scale=ws_s[:, P * n : P * (n + 1)],
+                rhs=short_w[u][:].bitcast(E5M2X4), rhs_scale=short_s[u][:], start=first, stop=not first,
+            )
 
-        def empty(on_vector, u, n):
-            if on_vector:
-                nc.vector.tensor_copy(p[u][n][:], res[u][n][:])
-            else:
-                nc.scalar.copy(p[u][n][:], res[u][n][:])
+        def pass_with_wb(u, n, first):
+            nc.tensor.matmul_mx(
+                out=p_bank[u][n][:], lhsT=wb_w[:, 2 * P * n : 2 * P * (n + 1)].bitcast(E2M1X4),
+                lhsT_scale=wb_s[:, P * n : P * (n + 1)],
+                rhs=hid_w[u][:].bitcast(E4M3X4), rhs_scale=hid_s[u][:], start=first, stop=not first,
+            )
 
-        def place(on_vector, u, n):
-            if on_vector:
-                nc.vector.tensor_copy(pages[n][:].indirect(half(idx5, u)), p[u][n][:])
-            else:
-                nc.scalar.activation(pages[n][:].indirect(half(idx5, u)), p[u][n][:], ACT.Copy)
+        def scatter_on_scalar(u, n):
+            nc.scalar.activation(pages[n][:].indirect(half_of(idx5, u)), p[u][n][:], ACT.Copy)
 
-        nc.vector.tensor_copy(xg4[:], xw[:].bitcast(U32).indirect(idx4[:]))
-        nc.vector.tensor_copy(xgs4[:], xs[:].indirect(idx4[:]))
+        gather_short_tokens(0)
+
         for t in range(PACK):
-            nc.scalar.copy(a[t][:, :J], acc[t][:])
+            nc.scalar.copy(a[t][:, :J], a_bank[t][:])
         for t in range(PACK):
-            gather(t < 2, g2[t][:], a[t][:], idx2[:])
+            look_up(t < VECTOR_PLANES_OF_A, partner[t][:], a[t][:], idx2[:])
         for t in range(PACK):
-            nc.vector.tensor_tensor(h[:, t, :], a[t][:, :J], g2[t][:], ALU.max)
-        short_way(0)
-        short_way(1)
-        g3pair = {}
-        g30 = sb("g30", [P, PACK, HALF], F32)
-        g3[0] = [g30[:, t, :] for t in range(PACK)]
-        g3pair[0] = [g30[:, 0:2, :], g30[:, 2:4, :]]
-        d[0] = sb("d0", [P, PACK, HALF], F32)
-        for t in range(PACK):
-            pick3(t == 2, t, 0)
-        subtract(0, 0, 2)
-        subtract(0, 2, 4)
-        g31 = [sb("g31%d" % k, [P, 2, HALF], F32, tag="g2%d" % (2 + k)) for k in range(2)]
-        g3[1] = [g31[t // 2][:, t % 2, :] for t in range(PACK)]
-        g3pair[1] = [g31[0][:], g31[1][:]]
-        d[1] = sb("d1", [P, PACK, HALF], F32, tag="g30")
-        for t in range(PACK):
-            pick3(t == 0, t, 1)
-        magnitude(0)
-        subtract(1, 0, 2)
-        subtract(1, 2, 4)
+            nc.vector.tensor_tensor(h1[:, t, :], a[t][:, :J], partner[t][:], ALU.max)
+        for n in PAGE_ORDER:
+            pass_with_ws(0, n, first=True)
+
+        other0 = sbuf("other0", [P, PACK, HALF], F32)
+        pairs0 = [other0[:, 0:2, :], other0[:, 2:4, :]]
+        diff0 = sbuf("diff0", [P, PACK, HALF], F32)
+        look_up_h1(0, pairs0)
+        subtract(0, pairs0, diff0)
+        other1 = [sbuf("other1%d" % i, [P, 2, HALF], F32, on_bytes_of="partner%d" % (2 + i)) for i in range(2)]
+        pairs1 = [other1[0][:], other1[1][:]]
+        diff1 = sbuf("diff1", [P, PACK, HALF], F32, on_bytes_of="other0")
+        look_up_h1(1, pairs1)
+        magnitude(0, diff0)
+        subtract(1, pairs1, diff1)
         quantise(0)
-        magnitude(1)
-        second(0)
+        magnitude(1, diff1)
+        for n in PAGE_ORDER:
+            pass_with_wb(0, n, first=False)
+
+        short_w.append(sbuf("short_w1", [P, HALF], U32, on_bytes_of="diff0"))
+        short_s.append(sbuf("short_s1", [P, HALF], U8, on_bytes_of="hid0"))
+        gather_short_tokens(1)
         quantise(1)
-        empty(False, 0, 1)
-        place(False, 0, 1)
-        empty(True, 0, 0)
-        second(1)
-        empty(True, 1, 1)
-        empty(True, 1, 0)
-        place(False, 0, 0)
-        place(True, 1, 1)
-        place(False, 1, 0)
+
+        nc.scalar.copy(p[0][1][:], p_bank[0][1][:])
+        scatter_on_scalar(0, 1)
+        nc.vector.tensor_copy(p[0][0][:], p_bank[0][0][:])
+        for n in PAGE_ORDER:
+            pass_with_wb(1, n, first=True)
+            pass_with_ws(1, n, first=False)
+        for n in PAGE_ORDER:
+            nc.vector.tensor_copy(p[1][n][:], p_bank[1][n][:])
+        scatter_on_scalar(0, 0)
+        nc.vector.tensor_copy(pages[1][:].indirect(half_of(idx5, 1)), p[1][1][:])
+        scatter_on_scalar(1, 0)
 
         nc.sync.dma_start(out[P : 2 * P, :], pages[1][:])
         nc.scalar.dma_start(out[0:P, :], pages[0][:])

@@ -77,11 +77,11 @@ def tile_list_passedon_solo_further_scattered_kernel(
 
         nc.sync.dma_start(idx[:], offs)
         nc.scalar.dma_start(xt_w[:], xt_words[0].rearrange("p c r -> p (c r)").bitcast(I32))
-        nc.gpsimd.dma_start(w_w[:].bitcast(I32), w_words[0].bitcast(I32))
+        nc.scalar.dma_start(w_w[:].bitcast(I32), w_words[0].bitcast(I32))
         for quadrant in range(P // QUADRANT):
             load_repeated_rows(nc.sync, xt_s, xt_scales[0], QUADRANT * quadrant, 4 * quadrant, 4, QUADRANT // 4)
-        load_repeated_rows(nc.scalar, w_s, w_scales[0], 0, 0, 14, 6)
-        load_repeated_rows(nc.sync, w_s, w_scales[0], 84, 12, 4, 11)
+        load_repeated_rows(nc.sync, w_s, w_scales[0], 0, 0, 14, 6)
+        load_repeated_rows(nc.gpsimd, w_s, w_scales[0], 84, 12, 4, 11)
         nc.sync.dma_start(idx4[:], offs4)
         nc.sync.dma_start(idx2[:], offs2)
         nc.sync.dma_start(idx3[:], offs3)
@@ -104,28 +104,22 @@ def tile_list_passedon_solo_further_scattered_kernel(
         for t in range(PACK):
             nc.scalar.copy(out=dealt_w[t][:].bitcast(U16), in_=w_w[:].bitcast(U16)[:, t::PACK])
 
-        def deal_scales(t):
-            nc.vector.tensor_copy(out=dealt_s[t][:], in_=w_s[:, t::PACK])
-
         xt_window = xt_w[:].bitcast(U32)
         tok_w = sbuf("tok_w", [P, J], U32)
         tok_s = sbuf("tok_s", [P, J], U8)
         short_w = [sbuf("short_w0", [P, HALF], U32)]
         short_s = [sbuf("short_s0", [P, HALF], U8)]
         nc.vector.tensor_copy(tok_s[:], xt_s[:].indirect(idx[:]))
-        nc.vector.tensor_copy(tok_w[:, slots(0)], xt_window.indirect(half_of(idx, 0)))
-        deal_scales(0)
-        nc.vector.tensor_copy(tok_w[:, slots(1)], xt_window.indirect(half_of(idx, 1)))
-        for t in range(1, PACK):
-            deal_scales(t)
+        nc.vector.tensor_copy(tok_w[:], xt_window.indirect(idx[:]))
+        for t in range(PACK):
+            nc.vector.tensor_copy(out=dealt_s[t][:], in_=w_s[:, t::PACK])
 
         a_bank = [psum.tile([P, J], F32, name="a_bank%d" % t) for t in range(PACK)]
         for t in range(PACK):
-            for u in range(2):
-                nc.tensor.matmul_mx(
-                    out=a_bank[t][:, slots(u)], lhsT=dealt_w[t][:].bitcast(E2M1X4), lhsT_scale=dealt_s[t][:],
-                    rhs=tok_w[:, slots(u)].bitcast(E5M2X4), rhs_scale=tok_s[:, slots(u)], start=True, stop=True,
-                )
+            nc.tensor.matmul_mx(
+                out=a_bank[t][:], lhsT=dealt_w[t][:].bitcast(E2M1X4), lhsT_scale=dealt_s[t][:],
+                rhs=tok_w[:].bitcast(E5M2X4), rhs_scale=tok_s[:], start=True, stop=True,
+            )
 
         p_bank = [[psum.tile([P, HALF], F32, name="p_bank%d%d" % (u, n)) for n in range(2)] for u in range(2)]
         partner = [sbuf("partner%d" % t, [P, J], F32) for t in range(PACK)]

from contextlib import ExitStack

import concourse.mybir as mybir

K, T, J, R, N, E = 512, 1024, 256, 512, 256, 1024
FLOPS = 2 * K * R * J + 2 * R * N * J + 2 * K * N * J

F32 = mybir.dt.float32
BF16 = mybir.dt.bfloat16
I32 = mybir.dt.int32
U32 = mybir.dt.uint32
U16 = mybir.dt.uint16
U8 = mybir.dt.uint8
E4M3X4 = mybir.dt.float8_e4m3fn_x4
E5M2X4 = mybir.dt.float8_e5m2_x4
E2M1X4 = mybir.dt.float4_e2m1fn_x4
ACT = mybir.ActivationFunctionType
ALU = mybir.AluOpType

P = 128
PACK = 4
QUADRANT = 32
HALF = J // 2
LIST_COLUMNS = J // 16
SPARE = 96
PAGE_ORDER = (1, 0)
VECTOR_PLANES_OF_A = 2
VECTOR_PLANE_OF_H1 = (2, 0)


def load_scale_rows(queue, tile, rows):
    words = rows.bitcast(I32)
    for quadrant in range(P // QUADRANT):
        first = QUADRANT * quadrant
        queue.dma_start(tile[first : first + 4, :].bitcast(I32), words[4 * quadrant : 4 * quadrant + 4, :])


def load_repeated_rows(queue, tile, rows, first_partition, first_row, count, copies):
    words = rows.bitcast(I32)[first_row : first_row + count, :]
    queue.dma_start(
        tile[first_partition : first_partition + count * copies, :].bitcast(I32),
        words.unsqueeze(0).broadcast_to([copies, count, words.shape[1]]),
    )


def tile_list_passedon_solo_further_scattered_kernel(
    tc, xt_words, xt_scales, w_words, w_scales, wb_words, wb_scales, ws_words, ws_scales,
    offs, offs2, offs3, offs4, offs5, out
):
    nc = tc.nc
    with ExitStack() as ctx:
        keep = ctx.enter_context(tc.tile_pool(name="keep", bufs=1))
        psum = ctx.enter_context(tc.psum_pool(name="psum", bufs=1))

        def sbuf(name, shape, dtype, on_bytes_of=None):
            return keep.tile(shape, dtype, name=name, tag=on_bytes_of or name, align_bytes=64)

        def half_of(offsets, u):
            return offsets[:, u * LIST_COLUMNS // 2 : (u + 1) * LIST_COLUMNS // 2]

        def slots(u):
            return slice(HALF * u, HALF * (u + 1))

        idx = sbuf("idx", [P, LIST_COLUMNS], U16)
        idx2 = sbuf("idx2", [P, LIST_COLUMNS], U16)
        idx3 = sbuf("idx3", [P, LIST_COLUMNS], U16)
        idx4 = sbuf("idx4", [P, LIST_COLUMNS], U16)
        idx5 = sbuf("idx5", [P, LIST_COLUMNS], U16)
        xt_w = sbuf("xt_w", [P, T], I32)
        xt_s = sbuf("xt_s", [P, T], U8)
        w_w = sbuf("w_w", [P, 2 * R], U8)
        w_s = sbuf("w_s", [P, R], U8)
        wb_w = sbuf("wb_w", [P, 2 * N], U8)
        wb_s = sbuf("wb_s", [P, N], U8)
        ws_w = sbuf("ws_w", [P, 2 * N], U8)
        ws_s = sbuf("ws_s", [P, N], U8)

        nc.sync.dma_start(idx[:], offs)
        nc.scalar.dma_start(xt_w[:], xt_words[0].rearrange("p c r -> p (c r)").bitcast(I32))
        nc.scalar.dma_start(w_w[:].bitcast(I32), w_words[0].bitcast(I32))
        for quadrant in range(P // QUADRANT):
            load_repeated_rows(nc.sync, xt_s, xt_scales[0], QUADRANT * quadrant, 4 * quadrant, 4, QUADRANT // 4)
        load_repeated_rows(nc.sync, w_s, w_scales[0], 0, 0, 14, 6)
        load_repeated_rows(nc.gpsimd, w_s, w_scales[0], 84, 12, 4, 11)
        nc.sync.dma_start(idx4[:], offs4)
        nc.sync.dma_start(idx2[:], offs2)
        nc.sync.dma_start(idx3[:], offs3)
        nc.sync.dma_start(ws_w[:].bitcast(I32), ws_words[0].bitcast(I32))
        load_scale_rows(nc.sync, ws_s, ws_scales[0])
        nc.sync.dma_start(wb_w[:].bitcast(I32), wb_words[0].bitcast(I32))
        load_scale_rows(nc.sync, wb_s, wb_scales[0])
        nc.sync.dma_start(idx5[:], offs5)

        pages = [sbuf("page%d" % n, [P, E], F32) for n in range(2)]
        a = [sbuf("a%d" % t, [P, J + SPARE], F32) for t in range(PACK)]
        for t in range(PACK):
            nc.gpsimd.memset(a[t][:, J:], 0.0)
        nc.gpsimd.memset(pages[0][:], 0.0)
        nc.vector.memset(pages[1][:, : E - 1], 0.0)
        nc.vector.memset(pages[1][:, E - 1 :], 0.0)

        dealt_w = [sbuf("dealt_w%d" % t, [P, 2 * P], U8) for t in range(PACK)]
        dealt_s = [sbuf("dealt_s%d" % t, [P, P], U8) for t in range(PACK)]
        for t in range(PACK):
            nc.scalar.copy(out=dealt_w[t][:].bitcast(U16), in_=w_w[:].bitcast(U16)[:, t::PACK])

        xt_window = xt_w[:].bitcast(U32)
        tok_w = sbuf("tok_w", [P, J], U32)
        tok_s = sbuf("tok_s", [P, J], U8)
        short_w = [sbuf("short_w0", [P, HALF], U32)]
        short_s = [sbuf("short_s0", [P, HALF], U8)]
        nc.vector.tensor_copy(tok_s[:], xt_s[:].indirect(idx[:]))
        nc.vector.tensor_copy(tok_w[:], xt_window.indirect(idx[:]))
        for t in range(PACK):
            nc.vector.tensor_copy(out=dealt_s[t][:], in_=w_s[:, t::PACK])

        a_bank = [psum.tile([P, J], F32, name="a_bank%d" % t) for t in range(PACK)]
        for t in range(PACK):
            nc.tensor.matmul_mx(
                out=a_bank[t][:], lhsT=dealt_w[t][:].bitcast(E2M1X4), lhsT_scale=dealt_s[t][:],
                rhs=tok_w[:].bitcast(E5M2X4), rhs_scale=tok_s[:], start=True, stop=True,
            )

        p_bank = [[psum.tile([P, HALF], F32, name="p_bank%d%d" % (u, n)) for n in range(2)] for u in range(2)]
        partner = [sbuf("partner%d" % t, [P, J], F32) for t in range(PACK)]
        h1 = sbuf("h1", [P, PACK, J], F32)
        hid = [sbuf("hid%d" % u, [P, HALF, PACK], BF16) for u in range(2)]
        hid_w = [sbuf("hid_w%d" % u, [P, HALF], U32) for u in range(2)]
        hid_s = [sbuf("hid_s%d" % u, [P, HALF], U8) for u in range(2)]
        p = [[sbuf("p%d%d" % (u, n), [P, HALF], F32) for n in range(2)] for u in range(2)]

        def gather_short_tokens(u):
            nc.vector.tensor_copy(short_w[u][:], xt_window.indirect(half_of(idx4, u)))
            nc.vector.tensor_copy(short_s[u][:], xt_s[:].indirect(half_of(idx4, u)))

        def look_up(on_vector, picked, window, offsets):
            if on_vector:
                nc.vector.tensor_copy(picked, window.indirect(offsets))
            else:
                nc.scalar.activation(picked, window.indirect(offsets), ACT.Copy)

        def look_up_h1(u, pairs):
            for t in range(PACK):
                look_up(t == VECTOR_PLANE_OF_H1[u], pairs[t // 2][:, t % 2, :], h1[:, t, :], half_of(idx3, u))

        def subtract(u, pairs, diff):
            for i in range(2):
                planes = slice(2 * i, 2 * i + 2)
                nc.vector.tensor_tensor(diff[:, planes, :], h1[:, planes, slots(u)], pairs[i], ALU.subtract)

        def magnitude(u, diff):
            nc.scalar.activation(
                hid[u][:].rearrange("q (c i) t -> q c t i", i=4),
                diff[:].rearrange("q t (c i) -> q c t i", i=4),
                ACT.Abs,
            )

        def quantise(u):
            nc.vector.quantize_mx(
                out=hid_w[u][:].bitcast(E4M3X4), scales=hid_s[u][:], in_=hid[u][:].rearrange("q j t -> q (j t)")
            )

        def pass_with_ws(u, n, first):
            nc.tensor.matmul_mx(
                out=p_bank[u][n][:], lhsT=ws_w[:, 2 * P * n : 2 * P * (n + 1)].bitcast(E2M1X4),
                lhsT_scale=ws_s[:, P * n : P * (n + 1)],
                rhs=short_w[u][:].bitcast(E5M2X4), rhs_scale=short_s[u][:], start=first, stop=not first,
            )

        def pass_with_wb(u, n, first):
            nc.tensor.matmul_mx(
                out=p_bank[u][n][:], lhsT=wb_w[:, 2 * P * n : 2 * P * (n + 1)].bitcast(E2M1X4),
                lhsT_scale=wb_s[:, P * n : P * (n + 1)],
                rhs=hid_w[u][:].bitcast(E4M3X4), rhs_scale=hid_s[u][:], start=first, stop=not first,
            )

        def scatter_on_scalar(u, n):
            nc.scalar.activation(pages[n][:].indirect(half_of(idx5, u)), p[u][n][:], ACT.Copy)

        gather_short_tokens(0)

        for t in range(PACK):
            nc.scalar.copy(a[t][:, :J], a_bank[t][:])
        for t in range(PACK):
            look_up(t < VECTOR_PLANES_OF_A, partner[t][:], a[t][:], idx2[:])
        for t in range(PACK):
            nc.vector.tensor_tensor(h1[:, t, :], a[t][:, :J], partner[t][:], ALU.max)
        for n in PAGE_ORDER:
            pass_with_ws(0, n, first=True)

        other0 = sbuf("other0", [P, PACK, HALF], F32)
        pairs0 = [other0[:, 0:2, :], other0[:, 2:4, :]]
        diff0 = sbuf("diff0", [P, PACK, HALF], F32)
        look_up_h1(0, pairs0)
        subtract(0, pairs0, diff0)
        other1 = [sbuf("other1%d" % i, [P, 2, HALF], F32, on_bytes_of="partner%d" % (2 + i)) for i in range(2)]
        pairs1 = [other1[0][:], other1[1][:]]
        diff1 = sbuf("diff1", [P, PACK, HALF], F32, on_bytes_of="other0")
        look_up_h1(1, pairs1)
        magnitude(0, diff0)
        subtract(1, pairs1, diff1)
        quantise(0)
        magnitude(1, diff1)
        for n in PAGE_ORDER:
            pass_with_wb(0, n, first=False)

        short_w.append(sbuf("short_w1", [P, HALF], U32, on_bytes_of="diff0"))
        short_s.append(sbuf("short_s1", [P, HALF], U8, on_bytes_of="hid0"))
        gather_short_tokens(1)
        quantise(1)

        nc.scalar.copy(p[0][1][:], p_bank[0][1][:])
        scatter_on_scalar(0, 1)
        nc.vector.tensor_copy(p[0][0][:], p_bank[0][0][:])
        for n in PAGE_ORDER:
            pass_with_wb(1, n, first=True)
            pass_with_ws(1, n, first=False)
        for n in PAGE_ORDER:
            nc.vector.tensor_copy(p[1][n][:], p_bank[1][n][:])
        scatter_on_scalar(0, 0)
        nc.vector.tensor_copy(pages[1][:].indirect(half_of(idx5, 1)), p[1][1][:])
        scatter_on_scalar(1, 0)

        nc.sync.dma_start(out[P : 2 * P, :], pages[1][:])
        nc.scalar.dma_start(out[0:P, :], pages[0][:])
